import numpy as np, ml_dtypes
CORES = [12,28,60,100,156,228]
N = 6
import mx_ref
NC, G = 128, 4
C = np.float32(0.019)
BF = ml_dtypes.bfloat16
def tile(rs):
    return np.stack(rs, axis=2).reshape(128, -1).astype(BF)
def act(Z):
    return [np.maximum(z, 0) * C for z in Z]
def pk(c, s, i=0):
    return (np.ascontiguousarray(c[:, 512 * i:512 * i + 512]), mx_ref.live(s[:, 128 * i:128 * i + 128]))
def inputs(rng, e, E):
    def f(*shape):
        v = (rng.standard_normal(shape, dtype=np.float32) * np.exp2(rng.integers(-2, 3, shape[:-1] + (1,)))).astype(BF)
        return mx_ref.spread((v.astype(np.float32) * np.exp2(rng.integers(-E, E + 1, shape[:-2] + (1, 1))).astype(np.float32)).astype(BF), rng, e)
    def packed(k):
        c = np.zeros((N, 128, k * 512), np.uint8); s = np.zeros((N, 128, k * 128), np.uint8)
        for r in range(N):
            for i in range(k):
                a, b = mx_ref.quantize(f(128, 512)); c[r][:, 512 * i:512 * i + 512] = a; s[r][:, 128 * i:128 * i + 128] = mx_ref.plane(b, rng)
        return c, s
    d = {}
    d["ac"], d["az"] = packed(1)
    d["bc"], d["bs"] = packed(1)
    d["cc"], d["cs"] = packed(1)
    d["x"] = f(N, 128, 4 * NC)
    return d
def setup_inputs(rng):
    return inputs(rng, 0, 0)
def setup_inputs_blocks(rng):
    return inputs(rng, 2, 0)
def setup_inputs_wide(rng):
    return inputs(rng, 0, 4)
def reference(ac, az, bc, bs, cc, cs, x):
    y = np.zeros((N, 128, N * NC), np.float32)
    for r in range(N):
        h = mx_ref.quantize(tile(act([mx_ref.matmul(pk(ac[i], az[i]), mx_ref.quantize(x[r])) for i in range(G)])))
        h = mx_ref.quantize(tile(act([mx_ref.matmul(pk(bc[i], bs[i]), h) for i in range(G)])))
        for j in range(N):
            y[r][:, NC * j:NC * j + NC] = mx_ref.matmul(pk(cc[j], cs[j]), h)
    return {"y": y}

@@ -1,0 +1,300 @@
+from concourse.bass import DstId, RemoteDMATransfer
+from concourse.mybir import dt, AluOpType
+
+CORES = [12, 28, 60, 100, 156, 228]
+N = 6
+G = 4
+W = 128
+SCALE = 0.019
+
+FAR = {0: (1, 3), 1: (2, 5), 2: (4, 5), 3: (0, 4), 4: (0, 1, 2, 3, 5), 5: (0, 1, 2, 3, 4)}
+
+PLACES = {"a": 1, "b": 1, "c": 2}
+BANKS = {"a": 2, "b": 2, "c": 4}
+TILES = {"a": G, "b": G, "c": N}
+KY = 2
+
+CODES = "float8_e4m3fn_x4"
+SCRATCH = {"yb": ("sbuf", [128, KY * W], "float32")}
+for _k in "xgh":
+    SCRATCH["t" + _k] = ("sbuf", [128, 4 * W], "bfloat16")
+    SCRATCH["q" + _k] = ("sbuf", [128, W], CODES)
+    SCRATCH["s" + _k] = ("sbuf", [128, W], "uint8")
+for _k in "abc":
+    SCRATCH["w" + _k] = ("sbuf", [128, PLACES[_k] * W], CODES)
+    SCRATCH["p" + _k] = ("sbuf", [128, PLACES[_k] * W], "uint8")
+    SCRATCH["z" + _k] = ("psum", [128, 512 * BANKS[_k]], "float32")
+    SCRATCH["d" + _k] = ("dram", [128, W], CODES)
+    for _j in range(TILES[_k]):
+        SCRATCH["l%s%d" % (_k, _j)] = ("dram", [128, W], CODES)
+SCRATCH["dp"] = ("dram", [128, W], "uint8")
+SCRATCH["dq"] = ("dram", [128, 2 * W], "uint8")
+SCRATCH["dr"] = ("dram", [128, W], "uint8")
+for _j in range(N):
+    if _j < G:
+        SCRATCH["lp%d" % _j] = ("dram", [128, W], "uint8")
+    SCRATCH["lq%d" % _j] = ("dram", [128, (2 if _j < G else 1) * W], "uint8")
+
+SEMAPHORES = ["out", "lx", "qx", "qg", "qh"]
+for _k in "apbqc":
+    SEMAPHORES += ["h" + _k, "s" + _k]
+    for _j in range(N):
+        SEMAPHORES.append("r%s%d" % (_k, _j))
+for _k in "abc":
+    for _j in range(TILES[_k]):
+        SEMAPHORES += ["l%s%d" % (_k, _j), "m%s%d" % (_k, _j), "e%s%d" % (_k, _j)]
+for _j in range(N):
+    SEMAPHORES.append("y%d" % _j)
+
+
+def _bits(m):
+    return [i for i in range(16) if m >> i & 1]
+
+
+def _alt(m):
+    return sum(1 << i for i in _bits(m)[::2])
+
+
+def _helpers(topo, s):
+    c = CORES[s]
+    chip = [k for k in range(256) if topo.host(k) == topo.host(c) and topo.chip(k) == topo.chip(c) and k != c]
+    mate = [k for k in range(256) if topo.mates(c, k)][0]
+    able = [k for k in chip if topo.may_write(k, mate)]
+    return ([k for k in able if topo.die(k) == topo.die(c)][0], [k for k in able if topo.die(k) != topo.die(c)][0])
+
+
+def _plan(topo, s, k):
+    c = CORES[s]
+    near, far = _helpers(topo, s)
+    send = {c: [], near: [], far: []}
+    for d in range(N):
+        if d != s:
+            if k in "ap" and topo.may_write(c, CORES[d]):
+                send[c].append(d)
+            elif d in FAR[s]:
+                send[far].append(d)
+            else:
+                send[near].append(d)
+    return send
+
+
+def _pieces(s):
+    return "apbqc" if s < G else "qc"
+
+
+def _off_mask(topo, src, dests):
+    m = 0xFFFF
+    for d in dests:
+        m &= topo.mask(src, CORES[d])
+    return _alt(m) if src in CORES or len(dests) < 2 else m
+
+
+def _chip_mask(topo, c, helper):
+    m = topo.mask(c, helper)
+    for d in CORES:
+        if d != c:
+            m &= ~topo.mask(c, d)
+    return m
+
+
+def _dst(topo, src, core):
+    rid, pid = topo.addr(core, src)
+    return DstId(rid=rid, pnc=pid)
+
+
+def _u8(t):
+    return t[:].bitcast(dt.uint8)
+
+
+def _src(T, s, k):
+    if k == "p":
+        return T.dp[:]
+    if k == "q":
+        return T.dq[:] if s < G else T.dr[:]
+    return _u8(T["d" + k])
+
+
+def _land(T, s, k):
+    t = T["l%s%d" % (k, s)]
+    return t[:] if k in "pq" else _u8(t)
+
+
+def _away(T, topo, src, s, k):
+    dests = _plan(topo, s, k)[src]
+    m = _off_mask(topo, src, dests)
+    return RemoteDMATransfer(dst_ids=[_dst(topo, src, CORES[d]) for d in dests], dma_engine_mask=m,
+                             remote_sem=T.sem["r%s%d" % (k, s)], srcs=[_src(T, s, k)],
+                             dsts=[_land(T, s, k) for d in dests], alu_op=0), len(_bits(m))
+
+
+def rank_program(g, core, T, topo):
+    rank = T.rank_of(core)
+    if rank is not None:
+        _sends(g, core, T, topo, rank)
+        _compute(g, core, T, topo, rank)
+        return
+    for s in range(N):
+        if core in _helpers(topo, s):
+            _helper(g, core, T, topo, s)
+
+
+def _came(topo, r, s, k):
+    for src, dests in _plan(topo, s, k).items():
+        if r in dests:
+            return len(_bits(_off_mask(topo, src, dests))), (1 if src == CORES[s] else 2)
+
+
+def _helper(g, core, T, topo, s):
+    n = len(_bits(_chip_mask(topo, CORES[s], core)))
+    sent = 0
+    for k in _pieces(s):
+        if _plan(topo, s, k)[core]:
+            g.wait_ge(T.sem["h" + k], n)
+            t, e = _away(T, topo, core, s, k)
+            g.remote_dma_fused([t], local_sem=T.sem.out)
+            sent += e
+    if sent:
+        g.wait_ge(T.sem.out, sent)
+
+
+def _sends(g, core, T, topo, r):
+    sem = T.sem
+    sent = [0]
+
+    def inside(k):
+        to = [h for h in _helpers(topo, r) if _plan(topo, r, k)[h]]
+        m = _chip_mask(topo, core, to[0])
+        sent[0] += len(_bits(m))
+        g.remote_dma_fused([RemoteDMATransfer(dst_ids=[_dst(topo, core, h) for h in to], dma_engine_mask=m,
+                                              remote_sem=sem["h" + k], srcs=[_src(T, r, k)],
+                                              dsts=[_src(T, r, k) for h in to], alu_op=0)], local_sem=sem.out)
+
+    def away(k):
+        t, e = _away(T, topo, core, r, k)
+        sent[0] += e
+        g.remote_dma_fused([t], local_sem=sem.out)
+
+    if r < G:
+        g.wait_ge(sem.sa, 16)
+        inside("a")
+        g.wait_ge(sem.sp, 16)
+        inside("p")
+        away("a")
+        away("p")
+        g.wait_ge(sem.sb, 16)
+        inside("b")
+        g.wait_ge(sem.sq, 32)
+        inside("q")
+        g.wait_ge(sem.sc, 16)
+        inside("c")
+    else:
+        first = [s for s in range(G) if _came(topo, r, s, "a")[1] == 1][0]
+        g.wait_ge(sem["ra%d" % first], _came(topo, r, first, "a")[0])
+        g.wait_ge(sem.sq, 16)
+        inside("q")
+        g.wait_ge(sem.sc, 16)
+        inside("c")
+    g.wait_ge(sem.out, sent[0])
+
+
+def _compute(g, core, T, topo, r):
+    sem, sync, scalar, vector, tensor = T.sem, g.sync, g.scalar, g.vector, g.tensor
+    plane_in = {"a": T.az, "b": T.bs, "c": T.cs}
+
+    order = {}
+    for k in "abc":
+        n = TILES[k]
+        own = [r] if r < n else []
+        order[k] = own + sorted([s for s in range(n) if s != r], key=lambda s: (_came(topo, r, s, k)[1], s))
+
+    def codes(k, i):
+        s, a = order[k][i], W * (i % PLACES[k])
+        if i >= PLACES[k]:
+            sync.wait_ge(sem["m%s%d" % (k, i - PLACES[k])], 1)
+        if s == r:
+            src = T[k + "c"][:]
+        else:
+            sync.wait_ge(sem["r%s%d" % (k, s)], _came(topo, r, s, k)[0])
+            src = _land(T, s, k)
+        sync.dma_start(T["w" + k][:, a:a + W].bitcast(dt.uint8), src).then_inc(sem["l%s%d" % (k, i)], 16)
+
+    def plane(k, i):
+        s, a = order[k][i], W * (i % PLACES[k])
+        if i >= PLACES[k]:
+            scalar.wait_ge(sem["m%s%d" % (k, i - PLACES[k])], 1)
+        if s == r:
+            src = plane_in[k][:]
+        else:
+            p = "p" if k == "a" else "q"
+            scalar.wait_ge(sem["r%s%d" % (p, s)], _came(topo, r, s, p)[0])
+            o = W if k == "c" and s < G else 0
+            src = T["l%s%d" % (p, s)][:, o:o + W]
+        scalar.dma_start(T["p" + k][:, a:a + W], src).then_inc(sem["l%s%d" % (k, i)], 16)
+
+    def store(q, i):
+        q.wait_ge(sem["ec%d" % i], 1)
+        s, a = order["c"][i], W * (i % KY)
+        q.dma_start(T.y[:, W * s:W * s + W], T.yb[:, a:a + W]).then_inc(sem["y%d" % i], 16)
+
+    own = 1 if r < G else 0
+    if r < G:
+        sync.dma_start(_u8(T.da), T.ac[:]).then_inc(sem.sa, 16)
+        codes("a", 0)
+        sync.dma_start(_u8(T.db), T.bc[:]).then_inc(sem.sb, 16)
+        codes("b", 0)
+    sync.dma_start(_u8(T.dc), T.cc[:]).then_inc(sem.sc, 16)
+    codes("c", 0)
+    if r < G:
+        scalar.dma_start(T.dp[:], T.az[:]).then_inc(sem.sp, 16)
+        scalar.dma_start(T.tx[:], T.x[:]).then_inc(sem.lx, 16)
+        plane("a", 0)
+        scalar.dma_start(T.dq[:, 0:W], T.bs[:]).then_inc(sem.sq, 16)
+        scalar.dma_start(T.dq[:, W:2 * W], T.cs[:]).then_inc(sem.sq, 16)
+        plane("b", 0)
+    else:
+        scalar.dma_start(T.tx[:], T.x[:]).then_inc(sem.lx, 16)
+        scalar.dma_start(T.dr[:], T.cs[:]).then_inc(sem.sq, 16)
+    plane("c", 0)
+    for k, first in (("a", own), ("b", own), ("c", 1)):
+        last = TILES[k] if k != "c" else 2
+        for i in range(first, last):
+            codes(k, i)
+            plane(k, i)
+    for i in range(2, N, 2):
+        for j in (i, i + 1):
+            codes("c", j)
+            plane("c", j)
+        store(sync, i - 2)
+        store(scalar, i - 1)
+    store(sync, N - 2)
+    store(scalar, N - 1)
+    for i in range(N):
+        sync.wait_ge(sem["y%d" % i], 16)
+
+    vector.wait_ge(sem.lx, 16)
+    vector.quantize_mx(T.qx[:], T.sx[:], T.tx[:]).then_inc(sem.qx, 1)
+    for k, t, c, p, q in (("a", T.tg, T.qg, T.sg, "qg"), ("b", T.th, T.qh, T.sh, "qh")):
+        for i in range(G):
+            s, b = order[k][i], 512 * (i % BANKS[k])
+            vector.wait_ge(sem["m%s%d" % (k, i)], 1)
+            vector.tensor_scalar(t[:, s:4 * W:4], T["z" + k][:, b:b + W], 0.0, SCALE, AluOpType.max,
+                                 AluOpType.mult).then_inc(sem["e%s%d" % (k, i)], 1)
+        for i in range(G):
+            vector.wait_ge(sem["e%s%d" % (k, i)], 1)
+        vector.quantize_mx(c[:], p[:], t[:]).then_inc(sem[q], 1)
+    for i in range(N):
+        a, b = W * (i % KY), 512 * (i % BANKS["c"])
+        vector.wait_ge(sem["mc%d" % i], 1)
+        if i >= KY:
+            vector.wait_ge(sem["y%d" % (i - KY)], 16)
+        vector.tensor_copy(T.yb[:, a:a + W], T.zc[:, b:b + W]).then_inc(sem["ec%d" % i], 1)
+
+    for k, c, p, q in (("a", T.qx, T.sx, "qx"), ("b", T.qg, T.sg, "qg"), ("c", T.qh, T.sh, "qh")):
+        tensor.wait_ge(sem[q], 1)
+        for i in range(TILES[k]):
+            a, b = W * (i % PLACES[k]), 512 * (i % BANKS[k])
+            tensor.wait_ge(sem["l%s%d" % (k, i)], 32)
+            if i >= BANKS[k]:
+                tensor.wait_ge(sem["e%s%d" % (k, i - BANKS[k])], 1)
+            tensor.matmul_mx(T["z" + k][:, b:b + W], T["w" + k][:, a:a + W], T["p" + k][:, a:a + W], c[:], p[:], True,
+                             True).then_inc(sem["m%s%d" % (k, i)], 1)

@@ -7,12 +7,16 @@ G = 4
 W = 128
 SCALE = 0.019
 
-FAR = {0: (1, 3), 1: (2, 5), 2: (4, 5), 3: (0, 4), 4: (0, 1, 2, 3, 5), 5: (0, 1, 2, 3, 4)}
+LEAD = [0, 0, 0, 1, 1, 1]
+FIRST = {0: (4, 2, 1, 3, 5), 1: (0, 2, 4, 5, 3), 2: (1, 0, 4, 5, 3), 3: (5, 4, 0, 1, 2)}
+LANDED = {4: 0, 5: 3}
 
 PLACES = {"a": 1, "b": 1, "c": 2}
+PLANES = {"a": 2, "b": 2, "c": 2}
 BANKS = {"a": 2, "b": 2, "c": 4}
 TILES = {"a": G, "b": G, "c": N}
 KY = 2
+FEW = {"in": "apqbc", "help": "ap", "rank": ""}
 
 CODES = "float8_e4m3fn_x4"
 SCRATCH = {"yb": ("sbuf", [128, KY * W], "float32")}
@@ -22,7 +26,7 @@ for _k in "xgh":
     SCRATCH["s" + _k] = ("sbuf", [128, W], "uint8")
 for _k in "abc":
     SCRATCH["w" + _k] = ("sbuf", [128, PLACES[_k] * W], CODES)
-    SCRATCH["p" + _k] = ("sbuf", [128, PLACES[_k] * W], "uint8")
+    SCRATCH["p" + _k] = ("sbuf", [128, PLANES[_k] * W], "uint8")
     SCRATCH["z" + _k] = ("psum", [128, 512 * BANKS[_k]], "float32")
     SCRATCH["d" + _k] = ("dram", [128, W], CODES)
     for _j in range(TILES[_k]):
@@ -42,7 +46,7 @@ for _k in "apbqc":
         SEMAPHORES.append("r%s%d" % (_k, _j))
 for _k in "abc":
     for _j in range(TILES[_k]):
-        SEMAPHORES += ["l%s%d" % (_k, _j), "m%s%d" % (_k, _j), "e%s%d" % (_k, _j)]
+        SEMAPHORES += ["l%s%d" % (_k, _j), "n%s%d" % (_k, _j), "m%s%d" % (_k, _j), "e%s%d" % (_k, _j)]
 for _j in range(N):
     SEMAPHORES.append("y%d" % _j)
 
@@ -67,34 +71,31 @@ def _plan(topo, s, k):
     c = CORES[s]
     near, far = _helpers(topo, s)
     send = {c: [], near: [], far: []}
-    for d in range(N):
-        if d != s:
-            if k in "ap" and topo.may_write(c, CORES[d]):
-                send[c].append(d)
-            elif d in FAR[s]:
-                send[far].append(d)
-            else:
-                send[near].append(d)
+    for d in FIRST[s] if k in "ap" else [(s + 1 + i) % N for i in range(N - 1)]:
+        if k in "ap" and topo.may_write(c, CORES[d]):
+            send[c].append(d)
+        else:
+            send[(near, far)[LEAD[s] if k in "ap" else 1 - LEAD[s]]].append(d)
     return send
 
 
 def _pieces(s):
-    return "apbqc" if s < G else "qc"
+    return "paqbc" if s < G else "qc"
 
 
-def _off_mask(topo, src, dests):
+def _off_mask(topo, src, k, dests):
     m = 0xFFFF
     for d in dests:
         m &= topo.mask(src, CORES[d])
-    return _alt(m) if src in CORES or len(dests) < 2 else m
+    return _alt(m) if k in FEW["rank" if src in CORES else "help"] else m
 
 
-def _chip_mask(topo, c, helper):
+def _chip_mask(topo, c, k, helper):
     m = topo.mask(c, helper)
     for d in CORES:
         if d != c:
             m &= ~topo.mask(c, d)
-    return m
+    return _alt(m) if k in FEW["in"] else m
 
 
 def _dst(topo, src, core):
@@ -114,17 +115,19 @@ def _src(T, s, k):
     return _u8(T["d" + k])
 
 
-def _land(T, s, k):
+def _land(T, s, k, d):
+    if k in "ap" and LANDED.get(d) == s:
+        return T.wa[:, 0:W].bitcast(dt.uint8) if k == "a" else T.pa[:, 0:W]
     t = T["l%s%d" % (k, s)]
     return t[:] if k in "pq" else _u8(t)
 
 
 def _away(T, topo, src, s, k):
     dests = _plan(topo, s, k)[src]
-    m = _off_mask(topo, src, dests)
+    m = _off_mask(topo, src, k, dests)
     return RemoteDMATransfer(dst_ids=[_dst(topo, src, CORES[d]) for d in dests], dma_engine_mask=m,
                              remote_sem=T.sem["r%s%d" % (k, s)], srcs=[_src(T, s, k)],
-                             dsts=[_land(T, s, k) for d in dests], alu_op=0), len(_bits(m))
+                             dsts=[_land(T, s, k, d) for d in dests], alu_op=0), len(_bits(m))
 
 
 def rank_program(g, core, T, topo):
@@ -141,15 +144,14 @@ def rank_program(g, core, T, topo):
 def _came(topo, r, s, k):
     for src, dests in _plan(topo, s, k).items():
         if r in dests:
-            return len(_bits(_off_mask(topo, src, dests))), (1 if src == CORES[s] else 2)
+            return len(_bits(_off_mask(topo, src, k, dests))), (1 if src == CORES[s] else 2), dests.index(r)
 
 
 def _helper(g, core, T, topo, s):
-    n = len(_bits(_chip_mask(topo, CORES[s], core)))
     sent = 0
     for k in _pieces(s):
         if _plan(topo, s, k)[core]:
-            g.wait_ge(T.sem["h" + k], n)
+            g.wait_ge(T.sem["h" + k], len(_bits(_chip_mask(topo, CORES[s], k, core))))
             t, e = _away(T, topo, core, s, k)
             g.remote_dma_fused([t], local_sem=T.sem.out)
             sent += e
@@ -163,7 +165,7 @@ def _sends(g, core, T, topo, r):
 
     def inside(k):
         to = [h for h in _helpers(topo, r) if _plan(topo, r, k)[h]]
-        m = _chip_mask(topo, core, to[0])
+        m = _chip_mask(topo, core, k, to[0])
         sent[0] += len(_bits(m))
         g.remote_dma_fused([RemoteDMATransfer(dst_ids=[_dst(topo, core, h) for h in to], dma_engine_mask=m,
                                               remote_sem=sem["h" + k], srcs=[_src(T, r, k)],
@@ -175,20 +177,20 @@ def _sends(g, core, T, topo, r):
         g.remote_dma_fused([t], local_sem=sem.out)
 
     if r < G:
-        g.wait_ge(sem.sa, 16)
-        inside("a")
         g.wait_ge(sem.sp, 16)
         inside("p")
-        away("a")
+        g.wait_ge(sem.sa, 16)
+        inside("a")
         away("p")
-        g.wait_ge(sem.sb, 16)
-        inside("b")
+        away("a")
         g.wait_ge(sem.sq, 32)
         inside("q")
+        g.wait_ge(sem.sb, 16)
+        inside("b")
         g.wait_ge(sem.sc, 16)
         inside("c")
     else:
-        first = [s for s in range(G) if _came(topo, r, s, "a")[1] == 1][0]
+        first = LANDED[r]
         g.wait_ge(sem["ra%d" % first], _came(topo, r, first, "a")[0])
         g.wait_ge(sem.sq, 16)
         inside("q")
@@ -203,25 +205,28 @@ def _compute(g, core, T, topo, r):
 
     order = {}
     for k in "abc":
-        n = TILES[k]
-        own = [r] if r < n else []
-        order[k] = own + sorted([s for s in range(n) if s != r], key=lambda s: (_came(topo, r, s, k)[1], s))
+        own = [r] if r < TILES[k] else [LANDED[r]] if k == "a" else []
+        order[k] = own + sorted([s for s in range(TILES[k]) if s not in own], key=lambda s: _came(topo, r, s, k)[1:] + (s,))
 
     def codes(k, i):
         s, a = order[k][i], W * (i % PLACES[k])
+        if k == "a" and LANDED.get(r) == s:
+            return
         if i >= PLACES[k]:
             sync.wait_ge(sem["m%s%d" % (k, i - PLACES[k])], 1)
         if s == r:
             src = T[k + "c"][:]
         else:
             sync.wait_ge(sem["r%s%d" % (k, s)], _came(topo, r, s, k)[0])
-            src = _land(T, s, k)
+            src = _land(T, s, k, r)
         sync.dma_start(T["w" + k][:, a:a + W].bitcast(dt.uint8), src).then_inc(sem["l%s%d" % (k, i)], 16)
 
     def plane(k, i):
-        s, a = order[k][i], W * (i % PLACES[k])
-        if i >= PLACES[k]:
-            scalar.wait_ge(sem["m%s%d" % (k, i - PLACES[k])], 1)
+        s, a = order[k][i], W * (i % PLANES[k])
+        if k == "a" and LANDED.get(r) == s:
+            return
+        if i >= PLANES[k]:
+            scalar.wait_ge(sem["m%s%d" % (k, i - PLANES[k])], 1)
         if s == r:
             src = plane_in[k][:]
         else:
@@ -229,7 +234,7 @@ def _compute(g, core, T, topo, r):
             scalar.wait_ge(sem["r%s%d" % (p, s)], _came(topo, r, s, p)[0])
             o = W if k == "c" and s < G else 0
             src = T["l%s%d" % (p, s)][:, o:o + W]
-        scalar.dma_start(T["p" + k][:, a:a + W], src).then_inc(sem["l%s%d" % (k, i)], 16)
+        scalar.dma_start(T["p" + k][:, a:a + W], src).then_inc(sem["n%s%d" % (k, i)], 16)
 
     def store(q, i):
         q.wait_ge(sem["ec%d" % i], 1)
@@ -239,35 +244,38 @@ def _compute(g, core, T, topo, r):
     own = 1 if r < G else 0
     if r < G:
         sync.dma_start(_u8(T.da), T.ac[:]).then_inc(sem.sa, 16)
-        codes("a", 0)
-        sync.dma_start(_u8(T.db), T.bc[:]).then_inc(sem.sb, 16)
-        codes("b", 0)
-    sync.dma_start(_u8(T.dc), T.cc[:]).then_inc(sem.sc, 16)
-    codes("c", 0)
-    if r < G:
         scalar.dma_start(T.dp[:], T.az[:]).then_inc(sem.sp, 16)
         scalar.dma_start(T.tx[:], T.x[:]).then_inc(sem.lx, 16)
+        codes("a", 0)
         plane("a", 0)
+        sync.dma_start(_u8(T.db), T.bc[:]).then_inc(sem.sb, 16)
         scalar.dma_start(T.dq[:, 0:W], T.bs[:]).then_inc(sem.sq, 16)
         scalar.dma_start(T.dq[:, W:2 * W], T.cs[:]).then_inc(sem.sq, 16)
-        plane("b", 0)
     else:
         scalar.dma_start(T.tx[:], T.x[:]).then_inc(sem.lx, 16)
+        sync.dma_start(_u8(T.dc), T.cc[:]).then_inc(sem.sc, 16)
         scalar.dma_start(T.dr[:], T.cs[:]).then_inc(sem.sq, 16)
-    plane("c", 0)
-    for k, first in (("a", own), ("b", own), ("c", 1)):
-        last = TILES[k] if k != "c" else 2
-        for i in range(first, last):
-            codes(k, i)
-            plane(k, i)
-    for i in range(2, N, 2):
-        for j in (i, i + 1):
-            codes("c", j)
-            plane("c", j)
-        store(sync, i - 2)
-        store(scalar, i - 1)
-    store(sync, N - 2)
-    store(scalar, N - 1)
+    for i in range(1, G):
+        codes("a", i)
+        plane("a", i)
+        if i == 1 and r < G:
+            sync.dma_start(_u8(T.dc), T.cc[:]).then_inc(sem.sc, 16)
+        if i == 2 and r < G:
+            codes("b", 0)
+            plane("b", 0)
+    for i in range(own, G):
+        codes("b", i)
+        plane("b", i)
+        if i >= G - KY:
+            codes("c", i - G + KY)
+            plane("c", i - G + KY)
+    for i in range(0, N, 2):
+        if i + 2 < N:
+            for j in (i + 2, i + 3):
+                codes("c", j)
+                plane("c", j)
+        store(sync, i)
+        store(scalar, i + 1)
     for i in range(N):
         sync.wait_ge(sem["y%d" % i], 16)
 
@@ -292,9 +300,15 @@ def _compute(g, core, T, topo, r):
     for k, c, p, q in (("a", T.qx, T.sx, "qx"), ("b", T.qg, T.sg, "qg"), ("c", T.qh, T.sh, "qh")):
         tensor.wait_ge(sem[q], 1)
         for i in range(TILES[k]):
-            a, b = W * (i % PLACES[k]), 512 * (i % BANKS[k])
-            tensor.wait_ge(sem["l%s%d" % (k, i)], 32)
+            s = order[k][i]
+            a, o, b = W * (i % PLACES[k]), W * (i % PLANES[k]), 512 * (i % BANKS[k])
+            if k == "a" and LANDED.get(r) == s:
+                tensor.wait_ge(sem["rp%d" % s], _came(topo, r, s, "p")[0])
+                tensor.wait_ge(sem["ra%d" % s], _came(topo, r, s, "a")[0])
+            else:
+                tensor.wait_ge(sem["n%s%d" % (k, i)], 16)
+                tensor.wait_ge(sem["l%s%d" % (k, i)], 16)
             if i >= BANKS[k]:
                 tensor.wait_ge(sem["e%s%d" % (k, i - BANKS[k])], 1)
-            tensor.matmul_mx(T["z" + k][:, b:b + W], T["w" + k][:, a:a + W], T["p" + k][:, a:a + W], c[:], p[:], True,
+            tensor.matmul_mx(T["z" + k][:, b:b + W], T["w" + k][:, a:a + W], T["p" + k][:, o:o + W], c[:], p[:], True,
                              True).then_inc(sem["m%s%d" % (k, i)], 1)

@@ -1,5 +1,5 @@
 from concourse.bass import DstId, RemoteDMATransfer
-from concourse.mybir import dt, AluOpType
+from concourse.mybir import dt, ActivationFunctionType, AluOpType
 
 CORES = [12, 28, 60, 100, 156, 228]
 N = 6
@@ -7,56 +7,58 @@ G = 4
 W = 128
 SCALE = 0.019
 
-LEAD = [0, 0, 0, 1, 1, 1]
-FIRST = {0: (4, 2, 1, 3, 5), 1: (0, 2, 4, 5, 3), 2: (1, 0, 4, 5, 3), 3: (5, 4, 0, 1, 2)}
-LANDED = {4: 0, 5: 3}
-
-PLACES = {"a": 1, "b": 1, "c": 2}
-PLANES = {"a": 2, "b": 2, "c": 2}
-BANKS = {"a": 2, "b": 2, "c": 4}
-TILES = {"a": G, "b": G, "c": N}
-KY = 2
-FEW = {"in": "apqbc", "help": "ap", "rank": ""}
+PAIRS = ((0, 4), (1, 2), (3, 5))
+LAYER = {}
+MATE = {}
+for _f, _s in PAIRS:
+    LAYER[_f], LAYER[_s] = "a", "b"
+    MATE[_f], MATE[_s] = _s, _f
+SERVE = {"a": (3, 1, 0), "b": (4, 2, 5)}
+ORDER = {0: (0, 1, 2, 3), 1: (1, 0, 2, 3), 3: (3, 0, 1, 2), 2: (2, 0, 1, 3), 4: (0, 1, 2, 3), 5: (3, 0, 1, 2)}
+PLACES = {"a": (0, 1, 0, 1), "b": (0, 1, 2, 3)}
+LANDED = {0: (1,), 1: (0,), 3: (0,), 2: (0, 1, 3), 4: (0, 1, 2, 3), 5: (3, 0, 1, 2)}
 
 CODES = "float8_e4m3fn_x4"
-SCRATCH = {"yb": ("sbuf", [128, KY * W], "float32")}
-for _k in "xgh":
-    SCRATCH["t" + _k] = ("sbuf", [128, 4 * W], "bfloat16")
+SCRATCH = {
+    "yb": ("sbuf", [128, 2 * W], "float32"),
+    "tx": ("sbuf", [128, 4 * W], "bfloat16"),
+    "tt": ("sbuf", [128, 4 * W], "bfloat16"),
+    "ww": ("sbuf", [128, 2 * W], CODES),
+    "pw": ("sbuf", [128, 2 * W], "uint8"),
+    "wc": ("sbuf", [128, 2 * W], CODES),
+    "pc": ("sbuf", [128, 2 * W], "uint8"),
+    "z0": ("psum", [128, 512 * 2], "float32"),
+    "z1": ("psum", [128, 512 * 4], "float32"),
+    "zc": ("psum", [128, 512 * 2], "float32"),
+}
+for _k in "xovwh":
     SCRATCH["q" + _k] = ("sbuf", [128, W], CODES)
     SCRATCH["s" + _k] = ("sbuf", [128, W], "uint8")
+PLANE = {"a": "p", "b": "q", "c": "r"}
 for _k in "abc":
-    SCRATCH["w" + _k] = ("sbuf", [128, PLACES[_k] * W], CODES)
-    SCRATCH["p" + _k] = ("sbuf", [128, PLANES[_k] * W], "uint8")
-    SCRATCH["z" + _k] = ("psum", [128, 512 * BANKS[_k]], "float32")
     SCRATCH["d" + _k] = ("dram", [128, W], CODES)
-    for _j in range(TILES[_k]):
+    SCRATCH["d" + PLANE[_k]] = ("dram", [128, W], "uint8")
+    for _j in range(N if _k == "c" else G):
         SCRATCH["l%s%d" % (_k, _j)] = ("dram", [128, W], CODES)
-SCRATCH["dp"] = ("dram", [128, W], "uint8")
-SCRATCH["dq"] = ("dram", [128, 2 * W], "uint8")
-SCRATCH["dr"] = ("dram", [128, W], "uint8")
-for _j in range(N):
-    if _j < G:
-        SCRATCH["lp%d" % _j] = ("dram", [128, W], "uint8")
-    SCRATCH["lq%d" % _j] = ("dram", [128, (2 if _j < G else 1) * W], "uint8")
+        SCRATCH["l%s%d" % (PLANE[_k], _j)] = ("dram", [128, W], "uint8")
+SCRATCH["lg"] = ("dram", [128, W], CODES)
+SCRATCH["lh"] = ("dram", [128, W], "uint8")
 
-SEMAPHORES = ["out", "lx", "qx", "qg", "qh"]
-for _k in "apbqc":
+SEMAPHORES = ["out", "gone", "lx", "qx", "q0", "q1", "lg", "ng"]
+for _k in "apbqcr":
     SEMAPHORES += ["h" + _k, "s" + _k]
     for _j in range(N):
         SEMAPHORES.append("r%s%d" % (_k, _j))
-for _k in "abc":
-    for _j in range(TILES[_k]):
-        SEMAPHORES += ["l%s%d" % (_k, _j), "n%s%d" % (_k, _j), "m%s%d" % (_k, _j), "e%s%d" % (_k, _j)]
+for _k in "ovwk":
+    SEMAPHORES += [_k + "c", _k + "p"]
+for _j in range(G):
+    SEMAPHORES += ["lw%d" % _j, "nw%d" % _j, "m0%d" % _j, "m1%d" % _j, "e0%d" % _j, "e1%d" % _j]
 for _j in range(N):
-    SEMAPHORES.append("y%d" % _j)
+    SEMAPHORES += ["lc%d" % _j, "nc%d" % _j, "mc%d" % _j, "ec%d" % _j, "y%d" % _j]
 
 
 def _bits(m):
     return [i for i in range(16) if m >> i & 1]
-
-
-def _alt(m):
-    return sum(1 << i for i in _bits(m)[::2])
 
 
 def _helpers(topo, s):
@@ -71,31 +73,33 @@ def _plan(topo, s, k):
     c = CORES[s]
     near, far = _helpers(topo, s)
     send = {c: [], near: [], far: []}
-    for d in FIRST[s] if k in "ap" else [(s + 1 + i) % N for i in range(N - 1)]:
-        if k in "ap" and topo.may_write(c, CORES[d]):
-            send[c].append(d)
-        else:
-            send[(near, far)[LEAD[s] if k in "ap" else 1 - LEAD[s]]].append(d)
+    if k in "cr":
+        b = s - s % 2
+        send[far] = [d for d in [(b + i) % N for i in range(N)] if d != s]
+    else:
+        for d in SERVE["a" if k in "ap" else "b"]:
+            if d != s:
+                send[c if topo.may_write(c, CORES[d]) else near if k in "ap" else far].append(d)
     return send
 
 
-def _pieces(s):
-    return "paqbc" if s < G else "qc"
-
-
-def _off_mask(topo, src, k, dests):
+def _off_mask(topo, src, dests):
     m = 0xFFFF
     for d in dests:
         m &= topo.mask(src, CORES[d])
-    return _alt(m) if k in FEW["rank" if src in CORES else "help"] else m
+    return m
 
 
-def _chip_mask(topo, c, k, helper):
+def _chip_mask(topo, c, helper):
     m = topo.mask(c, helper)
     for d in CORES:
         if d != c:
             m &= ~topo.mask(c, d)
-    return _alt(m) if k in FEW["in"] else m
+    return sum(1 << i for i in _bits(m)[::2])
+
+
+def _mate_mask(topo, r):
+    return topo.mask(CORES[r], CORES[MATE[r]])
 
 
 def _dst(topo, src, core):
@@ -107,27 +111,39 @@ def _u8(t):
     return t[:].bitcast(dt.uint8)
 
 
-def _src(T, s, k):
-    if k == "p":
-        return T.dp[:]
-    if k == "q":
-        return T.dq[:] if s < G else T.dr[:]
-    return _u8(T["d" + k])
+def _all(T, name, k):
+    return _u8(T[name]) if k in "abc" else T[name][:]
+
+
+def _place(T, i, r, codes):
+    if i >= 2:
+        return T[("q" if codes else "s") + "ow"[i - 2]][:]
+    return (T.ww if codes else T.pw)[:, W * i:W * i + W]
+
+
+def _place8(T, i, r, codes):
+    p = _place(T, i, r, codes)
+    return p.bitcast(dt.uint8) if codes else p
 
 
 def _land(T, s, k, d):
-    if k in "ap" and LANDED.get(d) == s:
-        return T.wa[:, 0:W].bitcast(dt.uint8) if k == "a" else T.pa[:, 0:W]
-    t = T["l%s%d" % (k, s)]
-    return t[:] if k in "pq" else _u8(t)
+    if k not in "cr" and s in LANDED[d]:
+        return _place8(T, PLACES[LAYER[d]][ORDER[d].index(s)], d, k in "ab")
+    return _all(T, "l%s%d" % (k, s), k)
 
 
 def _away(T, topo, src, s, k):
     dests = _plan(topo, s, k)[src]
-    m = _off_mask(topo, src, k, dests)
+    m = _off_mask(topo, src, dests)
     return RemoteDMATransfer(dst_ids=[_dst(topo, src, CORES[d]) for d in dests], dma_engine_mask=m,
-                             remote_sem=T.sem["r%s%d" % (k, s)], srcs=[_src(T, s, k)],
+                             remote_sem=T.sem["r%s%d" % (k, s)], srcs=[_all(T, "d" + k, k)],
                              dsts=[_land(T, s, k, d) for d in dests], alu_op=0), len(_bits(m))
+
+
+def _came(topo, r, s, k):
+    for src, dests in _plan(topo, s, k).items():
+        if r in dests:
+            return len(_bits(_off_mask(topo, src, dests)))
 
 
 def rank_program(g, core, T, topo):
@@ -141,17 +157,11 @@ def rank_program(g, core, T, topo):
             _helper(g, core, T, topo, s)
 
 
-def _came(topo, r, s, k):
-    for src, dests in _plan(topo, s, k).items():
-        if r in dests:
-            return len(_bits(_off_mask(topo, src, k, dests))), (1 if src == CORES[s] else 2), dests.index(r)
-
-
 def _helper(g, core, T, topo, s):
     sent = 0
-    for k in _pieces(s):
+    for k in "paqbrc" if s < G else "rc":
         if _plan(topo, s, k)[core]:
-            g.wait_ge(T.sem["h" + k], len(_bits(_chip_mask(topo, CORES[s], k, core))))
+            g.wait_ge(T.sem["h" + k], len(_bits(_chip_mask(topo, CORES[s], core))))
             t, e = _away(T, topo, core, s, k)
             g.remote_dma_fused([t], local_sem=T.sem.out)
             sent += e
@@ -165,150 +175,209 @@ def _sends(g, core, T, topo, r):
 
     def inside(k):
         to = [h for h in _helpers(topo, r) if _plan(topo, r, k)[h]]
-        m = _chip_mask(topo, core, k, to[0])
-        sent[0] += len(_bits(m))
-        g.remote_dma_fused([RemoteDMATransfer(dst_ids=[_dst(topo, core, h) for h in to], dma_engine_mask=m,
-                                              remote_sem=sem["h" + k], srcs=[_src(T, r, k)],
-                                              dsts=[_src(T, r, k) for h in to], alu_op=0)], local_sem=sem.out)
+        if to:
+            m = _chip_mask(topo, core, to[0])
+            sent[0] += len(_bits(m))
+            d = _all(T, "d" + k, k)
+            g.remote_dma_fused([RemoteDMATransfer(dst_ids=[_dst(topo, core, h) for h in to], dma_engine_mask=m,
+                                                  remote_sem=sem["h" + k], srcs=[d], dsts=[d for h in to],
+                                                  alu_op=0)], local_sem=sem.out)
 
     def away(k):
-        t, e = _away(T, topo, core, r, k)
-        sent[0] += e
-        g.remote_dma_fused([t], local_sem=sem.out)
+        if _plan(topo, r, k)[core]:
+            t, e = _away(T, topo, core, r, k)
+            sent[0] += e
+            g.remote_dma_fused([t], local_sem=sem.out)
 
+    def mate(src, plane, codes, name, local):
+        m = _mate_mask(topo, r)
+        to = _dst(topo, core, CORES[MATE[r]])
+        for s, d, n in ((T["s" + src][:], plane[:], name + "p"), (_u8(T["q" + src]), _u8(codes), name + "c")):
+            if local == "out":
+                sent[0] += len(_bits(m))
+            g.remote_dma_fused([RemoteDMATransfer(dst_ids=[to], dma_engine_mask=m, remote_sem=sem[n], srcs=[s], dsts=[d],
+                                                  alu_op=0)], local_sem=sem[local])
+
+    first = LAYER[r] == "a"
     if r < G:
         g.wait_ge(sem.sp, 16)
         inside("p")
         g.wait_ge(sem.sa, 16)
         inside("a")
+    if not first:
+        g.wait_ge(sem.qx, 1)
+        mate("x", T.so, T.qo, "o", "out")
+    if r < G:
         away("p")
         away("a")
-        g.wait_ge(sem.sq, 32)
-        inside("q")
-        g.wait_ge(sem.sb, 16)
-        inside("b")
-        g.wait_ge(sem.sc, 16)
-        inside("c")
-    else:
-        first = LANDED[r]
-        g.wait_ge(sem["ra%d" % first], _came(topo, r, first, "a")[0])
         g.wait_ge(sem.sq, 16)
         inside("q")
-        g.wait_ge(sem.sc, 16)
-        inside("c")
+        away("q")
+        g.wait_ge(sem.sb, 16)
+        inside("b")
+        away("b")
+    g.wait_ge(sem.sr, 16)
+    inside("r")
+    g.wait_ge(sem.sc, 16)
+    inside("c")
+    g.wait_ge(sem.q0, 1)
+    if first:
+        mate("v", T.sv, T.qv, "v", "out")
+        g.wait_ge(sem.q1, 1)
+        mate("w", T.lh, T.lg, "w", "out")
+    else:
+        mate("h", T.sh, T.qh, "k", "gone")
     g.wait_ge(sem.out, sent[0])
 
 
 def _compute(g, core, T, topo, r):
     sem, sync, scalar, vector, tensor = T.sem, g.sync, g.scalar, g.vector, g.tensor
-    plane_in = {"a": T.az, "b": T.bs, "c": T.cs}
+    k = LAYER[r]
+    first = k == "a"
+    got = len(_bits(_mate_mask(topo, MATE[r])))
 
-    order = {}
-    for k in "abc":
-        own = [r] if r < TILES[k] else [LANDED[r]] if k == "a" else []
-        order[k] = own + sorted([s for s in range(TILES[k]) if s not in own], key=lambda s: _came(topo, r, s, k)[1:] + (s,))
+    order, places = ORDER[r], PLACES[k]
+    order_c = []
+    for p in [(r // 2 - i) % (N // 2) for i in range(N // 2)]:
+        order_c += [2 * p, 2 * p + 1] if 2 * p + 1 != r else [2 * p + 1, 2 * p]
 
-    def codes(k, i):
-        s, a = order[k][i], W * (i % PLACES[k])
-        if k == "a" and LANDED.get(r) == s:
+    def tile(i):
+        s, p = order[i], places[i]
+        if s in LANDED[r]:
             return
-        if i >= PLACES[k]:
-            sync.wait_ge(sem["m%s%d" % (k, i - PLACES[k])], 1)
-        if s == r:
-            src = T[k + "c"][:]
-        else:
-            sync.wait_ge(sem["r%s%d" % (k, s)], _came(topo, r, s, k)[0])
-            src = _land(T, s, k, r)
-        sync.dma_start(T["w" + k][:, a:a + W].bitcast(dt.uint8), src).then_inc(sem["l%s%d" % (k, i)], 16)
+        for q, n, x, own in ((sync, "lw", k, T.ac if first else T.bc), (scalar, "nw", PLANE[k], T.az if first else T.bs)):
+            if s == r:
+                src = own[:]
+            else:
+                q.wait_ge(sem["r%s%d" % (x, s)], _came(topo, r, s, x))
+                src = _land(T, s, x, r)
+            for m in [m for m in range(i) if places[m] == p]:
+                q.wait_ge(sem["m0%d" % m], 1)
+                q.wait_ge(sem["m1%d" % m], 1)
+            q.dma_start(_place8(T, p, r, q is sync), src).then_inc(sem["%s%d" % (n, i)], 16)
 
-    def plane(k, i):
-        s, a = order[k][i], W * (i % PLANES[k])
-        if k == "a" and LANDED.get(r) == s:
-            return
-        if i >= PLANES[k]:
-            scalar.wait_ge(sem["m%s%d" % (k, i - PLANES[k])], 1)
-        if s == r:
-            src = plane_in[k][:]
+    def tile_c(i):
+        s, w = order_c[i], slice(W * (i % 2), W * (i % 2) + W)
+        for q, n, x, buf, own in ((sync, "lc", "c", T.wc[:, w].bitcast(dt.uint8), T.cc),
+                                  (scalar, "nc", "r", T.pc[:, w], T.cs)):
+            if s == r:
+                src = own[:]
+            else:
+                q.wait_ge(sem["r%s%d" % (x, s)], _came(topo, r, s, x))
+                src = _land(T, s, x, r)
+            if i >= 2:
+                q.wait_ge(sem["mc%d" % (i - 2)], 1)
+            q.dma_start(buf, src).then_inc(sem["%s%d" % (n, i)], 16)
+
+    def block(q, i):
+        a, b = W * (i % 2), 512 * (i % 2)
+        q.wait_ge(sem["mc%d" % i], 1)
+        if i >= 2:
+            q.wait_ge(sem["y%d" % (i - 2)], 16)
+        if q is vector:
+            c = q.tensor_copy(T.yb[:, a:a + W], T.zc[:, b:b + W])
         else:
-            p = "p" if k == "a" else "q"
-            scalar.wait_ge(sem["r%s%d" % (p, s)], _came(topo, r, s, p)[0])
-            o = W if k == "c" and s < G else 0
-            src = T["l%s%d" % (p, s)][:, o:o + W]
-        scalar.dma_start(T["p" + k][:, a:a + W], src).then_inc(sem["n%s%d" % (k, i)], 16)
+            c = q.activation(T.yb[:, a:a + W], T.zc[:, b:b + W], ActivationFunctionType.Copy)
+        c.then_inc(sem["ec%d" % i], 1)
 
     def store(q, i):
+        a, s = W * (i % 2), W * order_c[i]
         q.wait_ge(sem["ec%d" % i], 1)
-        s, a = order["c"][i], W * (i % KY)
-        q.dma_start(T.y[:, W * s:W * s + W], T.yb[:, a:a + W]).then_inc(sem["y%d" % i], 16)
+        q.dma_start(T.y[:, s:s + W], T.yb[:, a:a + W]).then_inc(sem["y%d" % i], 16)
 
-    own = 1 if r < G else 0
     if r < G:
         sync.dma_start(_u8(T.da), T.ac[:]).then_inc(sem.sa, 16)
         scalar.dma_start(T.dp[:], T.az[:]).then_inc(sem.sp, 16)
-        scalar.dma_start(T.tx[:], T.x[:]).then_inc(sem.lx, 16)
-        codes("a", 0)
-        plane("a", 0)
+    scalar.dma_start(T.tx[:], T.x[:]).then_inc(sem.lx, 16)
+    if r < G and first:
+        tile(0)
+    if r < G:
         sync.dma_start(_u8(T.db), T.bc[:]).then_inc(sem.sb, 16)
-        scalar.dma_start(T.dq[:, 0:W], T.bs[:]).then_inc(sem.sq, 16)
-        scalar.dma_start(T.dq[:, W:2 * W], T.cs[:]).then_inc(sem.sq, 16)
-    else:
-        scalar.dma_start(T.tx[:], T.x[:]).then_inc(sem.lx, 16)
-        sync.dma_start(_u8(T.dc), T.cc[:]).then_inc(sem.sc, 16)
-        scalar.dma_start(T.dr[:], T.cs[:]).then_inc(sem.sq, 16)
-    for i in range(1, G):
-        codes("a", i)
-        plane("a", i)
-        if i == 1 and r < G:
-            sync.dma_start(_u8(T.dc), T.cc[:]).then_inc(sem.sc, 16)
-        if i == 2 and r < G:
-            codes("b", 0)
-            plane("b", 0)
-    for i in range(own, G):
-        codes("b", i)
-        plane("b", i)
-        if i >= G - KY:
-            codes("c", i - G + KY)
-            plane("c", i - G + KY)
+        scalar.dma_start(T.dq[:], T.bs[:]).then_inc(sem.sq, 16)
+    sync.dma_start(_u8(T.dc), T.cc[:]).then_inc(sem.sc, 16)
+    scalar.dma_start(T.dr[:], T.cs[:]).then_inc(sem.sr, 16)
+    if r < G and not first:
+        tile(0)
+    if first:
+        for i in range(1, G):
+            tile(i)
+    tile_c(0)
+    tile_c(1)
+    if not first:
+        for q, n, x, buf, src in ((sync, "lg", "wc", _u8(T.qv), _u8(T.lg)), (scalar, "ng", "wp", T.sv[:], T.lh[:])):
+            q.wait_ge(sem[x], got)
+            for i in range(G):
+                q.wait_ge(sem["m0%d" % i], 1)
+            q.dma_start(buf, src).then_inc(sem[n], 16)
     for i in range(0, N, 2):
         if i + 2 < N:
-            for j in (i + 2, i + 3):
-                codes("c", j)
-                plane("c", j)
+            tile_c(i + 2)
+            tile_c(i + 3)
         store(sync, i)
+        block(scalar, i + 1)
         store(scalar, i + 1)
     for i in range(N):
         sync.wait_ge(sem["y%d" % i], 16)
 
     vector.wait_ge(sem.lx, 16)
     vector.quantize_mx(T.qx[:], T.sx[:], T.tx[:]).then_inc(sem.qx, 1)
-    for k, t, c, p, q in (("a", T.tg, T.qg, T.sg, "qg"), ("b", T.th, T.qh, T.sh, "qh")):
+    out = "vw" if first else "hh"
+    for j in range(2):
+        z, banks = (T.z0, T.z1)[j], (2, 4)[j]
+        if j:
+            vector.wait_ge(sem.q0, 1)
         for i in range(G):
-            s, b = order[k][i], 512 * (i % BANKS[k])
-            vector.wait_ge(sem["m%s%d" % (k, i)], 1)
-            vector.tensor_scalar(t[:, s:4 * W:4], T["z" + k][:, b:b + W], 0.0, SCALE, AluOpType.max,
-                                 AluOpType.mult).then_inc(sem["e%s%d" % (k, i)], 1)
+            s, b = order[i], 512 * (i % banks)
+            vector.wait_ge(sem["m%d%d" % (j, i)], 1)
+            vector.tensor_scalar(T.tt[:, s:4 * W:4], z[:, b:b + W], 0.0, SCALE, AluOpType.max,
+                                 AluOpType.mult).then_inc(sem["e%d%d" % (j, i)], 1)
         for i in range(G):
-            vector.wait_ge(sem["e%s%d" % (k, i)], 1)
-        vector.quantize_mx(c[:], p[:], t[:]).then_inc(sem[q], 1)
-    for i in range(N):
-        a, b = W * (i % KY), 512 * (i % BANKS["c"])
-        vector.wait_ge(sem["mc%d" % i], 1)
-        if i >= KY:
-            vector.wait_ge(sem["y%d" % (i - KY)], 16)
-        vector.tensor_copy(T.yb[:, a:a + W], T.zc[:, b:b + W]).then_inc(sem["ec%d" % i], 1)
+            vector.wait_ge(sem["e%d%d" % (j, i)], 1)
+        if j and not first:
+            vector.wait_ge(sem.gone, 2 * len(_bits(_mate_mask(topo, r))))
+        vector.quantize_mx(T["q" + out[j]][:], T["s" + out[j]][:], T.tt[:]).then_inc(sem["q%d" % j], 1)
+    for i in range(0, N, 2):
+        block(vector, i)
 
-    for k, c, p, q in (("a", T.qx, T.sx, "qx"), ("b", T.qg, T.sg, "qg"), ("c", T.qh, T.sh, "qh")):
-        tensor.wait_ge(sem[q], 1)
-        for i in range(TILES[k]):
-            s = order[k][i]
-            a, o, b = W * (i % PLACES[k]), W * (i % PLANES[k]), 512 * (i % BANKS[k])
-            if k == "a" and LANDED.get(r) == s:
-                tensor.wait_ge(sem["rp%d" % s], _came(topo, r, s, "p")[0])
-                tensor.wait_ge(sem["ra%d" % s], _came(topo, r, s, "a")[0])
+    moving = "xo" if first else "vv"
+    steps = ((0, 0), (0, 1), (1, 0), (1, 1), (2, 0), (3, 0), (2, 1), (3, 1)) if first else (
+        (0, 0), (1, 0), (2, 0), (3, 0), (0, 1), (1, 1), (2, 1), (3, 1))
+    seen = []
+    for i, j in steps:
+        if j not in seen:
+            seen.append(j)
+            if first and j == 0:
+                tensor.wait_ge(sem.qx, 1)
+            elif first or j == 0:
+                n = "o" if first else "v"
+                tensor.wait_ge(sem[n + "p"], got)
+                tensor.wait_ge(sem[n + "c"], got)
             else:
-                tensor.wait_ge(sem["n%s%d" % (k, i)], 16)
-                tensor.wait_ge(sem["l%s%d" % (k, i)], 16)
-            if i >= BANKS[k]:
-                tensor.wait_ge(sem["e%s%d" % (k, i - BANKS[k])], 1)
-            tensor.matmul_mx(T["z" + k][:, b:b + W], T["w" + k][:, a:a + W], T["p" + k][:, o:o + W], c[:], p[:], True,
-                             True).then_inc(sem["m%s%d" % (k, i)], 1)
+                tensor.wait_ge(sem.ng, 16)
+                tensor.wait_ge(sem.lg, 16)
+        s, p = order[i], places[i]
+        if j == 0:
+            if s in LANDED[r]:
+                for x in (PLANE[k], k):
+                    tensor.wait_ge(sem["r%s%d" % (x, s)], _came(topo, r, s, x))
+            else:
+                tensor.wait_ge(sem["nw%d" % i], 16)
+                tensor.wait_ge(sem["lw%d" % i], 16)
+        z, banks = (T.z0, T.z1)[j], (2, 4)[j]
+        if i >= banks:
+            tensor.wait_ge(sem["e%d%d" % (j, i - banks)], 1)
+        b = 512 * (i % banks)
+        tensor.matmul_mx(z[:, b:b + W], _place(T, p, r, True), _place(T, p, r, False), T["q" + moving[j]][:],
+                         T["s" + moving[j]][:], True, True).then_inc(sem["m%d%d" % (j, i)], 1)
+    if first:
+        tensor.wait_ge(sem.kp, got)
+        tensor.wait_ge(sem.kc, got)
+    else:
+        tensor.wait_ge(sem.q1, 1)
+    for i in range(N):
+        w, b = slice(W * (i % 2), W * (i % 2) + W), 512 * (i % 2)
+        tensor.wait_ge(sem["nc%d" % i], 16)
+        tensor.wait_ge(sem["lc%d" % i], 16)
+        if i >= 2:
+            tensor.wait_ge(sem["ec%d" % (i - 2)], 1)
+        tensor.matmul_mx(T.zc[:, b:b + W], T.wc[:, w], T.pc[:, w], T.qh[:], T.sh[:], True, True).then_inc(sem["mc%d" % i], 1)

from concourse.bass import DstId, RemoteDMATransfer
from concourse.mybir import dt, ActivationFunctionType, AluOpType

CORES = [12, 28, 60, 100, 156, 228]
N = 6
G = 4
W = 128
SCALE = 0.019

PAIRS = ((0, 4), (1, 2), (3, 5))
LAYER = {}
MATE = {}
for _f, _s in PAIRS:
    LAYER[_f], LAYER[_s] = "a", "b"
    MATE[_f], MATE[_s] = _s, _f
SERVE = {"a": (3, 1, 0), "b": (4, 2, 5)}
ORDER = {0: (0, 1, 2, 3), 1: (1, 0, 2, 3), 3: (3, 0, 1, 2), 2: (2, 0, 1, 3), 4: (0, 1, 2, 3), 5: (3, 0, 1, 2)}
PLACES = {"a": (0, 1, 0, 1), "b": (0, 1, 2, 3)}
LANDED = {0: (1,), 1: (0,), 3: (0,), 2: (0, 1, 3), 4: (0, 1, 2, 3), 5: (3, 0, 1, 2)}

CODES = "float8_e4m3fn_x4"
SCRATCH = {
    "yb": ("sbuf", [128, 2 * W], "float32"),
    "tx": ("sbuf", [128, 4 * W], "bfloat16"),
    "tt": ("sbuf", [128, 4 * W], "bfloat16"),
    "ww": ("sbuf", [128, 2 * W], CODES),
    "pw": ("sbuf", [128, 2 * W], "uint8"),
    "wc": ("sbuf", [128, 2 * W], CODES),
    "pc": ("sbuf", [128, 2 * W], "uint8"),
    "z0": ("psum", [128, 512 * 2], "float32"),
    "z1": ("psum", [128, 512 * 4], "float32"),
    "zc": ("psum", [128, 512 * 2], "float32"),
}
for _k in "xovwh":
    SCRATCH["q" + _k] = ("sbuf", [128, W], CODES)
    SCRATCH["s" + _k] = ("sbuf", [128, W], "uint8")
PLANE = {"a": "p", "b": "q", "c": "r"}
for _k in "abc":
    SCRATCH["d" + _k] = ("dram", [128, W], CODES)
    SCRATCH["d" + PLANE[_k]] = ("dram", [128, W], "uint8")
    for _j in range(N if _k == "c" else G):
        SCRATCH["l%s%d" % (_k, _j)] = ("dram", [128, W], CODES)
        SCRATCH["l%s%d" % (PLANE[_k], _j)] = ("dram", [128, W], "uint8")
SCRATCH["lg"] = ("dram", [128, W], CODES)
SCRATCH["lh"] = ("dram", [128, W], "uint8")

SEMAPHORES = ["out", "gone", "lx", "qx", "q0", "q1", "lg", "ng"]
for _k in "apbqcr":
    SEMAPHORES += ["h" + _k, "s" + _k]
    for _j in range(N):
        SEMAPHORES.append("r%s%d" % (_k, _j))
for _k in "ovwk":
    SEMAPHORES += [_k + "c", _k + "p"]
for _j in range(G):
    SEMAPHORES += ["lw%d" % _j, "nw%d" % _j, "m0%d" % _j, "m1%d" % _j, "e0%d" % _j, "e1%d" % _j]
for _j in range(N):
    SEMAPHORES += ["lc%d" % _j, "nc%d" % _j, "mc%d" % _j, "ec%d" % _j, "y%d" % _j]


def _bits(m):
    return [i for i in range(16) if m >> i & 1]


def _helpers(topo, s):
    c = CORES[s]
    chip = [k for k in range(256) if topo.host(k) == topo.host(c) and topo.chip(k) == topo.chip(c) and k != c]
    mate = [k for k in range(256) if topo.mates(c, k)][0]
    able = [k for k in chip if topo.may_write(k, mate)]
    return ([k for k in able if topo.die(k) == topo.die(c)][0], [k for k in able if topo.die(k) != topo.die(c)][0])


def _plan(topo, s, k):
    c = CORES[s]
    near, far = _helpers(topo, s)
    send = {c: [], near: [], far: []}
    if k in "cr":
        b = s - s % 2
        send[far] = [d for d in [(b + i) % N for i in range(N)] if d != s]
    else:
        for d in SERVE["a" if k in "ap" else "b"]:
            if d != s:
                send[c if topo.may_write(c, CORES[d]) else near if k in "ap" else far].append(d)
    return send


def _off_mask(topo, src, dests):
    m = 0xFFFF
    for d in dests:
        m &= topo.mask(src, CORES[d])
    return m


def _chip_mask(topo, c, helper):
    m = topo.mask(c, helper)
    for d in CORES:
        if d != c:
            m &= ~topo.mask(c, d)
    return sum(1 << i for i in _bits(m)[::2])


def _mate_mask(topo, r):
    return topo.mask(CORES[r], CORES[MATE[r]])


def _dst(topo, src, core):
    rid, pid = topo.addr(core, src)
    return DstId(rid=rid, pnc=pid)


def _u8(t):
    return t[:].bitcast(dt.uint8)


def _all(T, name, k):
    return _u8(T[name]) if k in "abc" else T[name][:]


def _place(T, i, r, codes):
    if i >= 2:
        return T[("q" if codes else "s") + "ow"[i - 2]][:]
    return (T.ww if codes else T.pw)[:, W * i:W * i + W]


def _place8(T, i, r, codes):
    p = _place(T, i, r, codes)
    return p.bitcast(dt.uint8) if codes else p


def _land(T, s, k, d):
    if k not in "cr" and s in LANDED[d]:
        return _place8(T, PLACES[LAYER[d]][ORDER[d].index(s)], d, k in "ab")
    return _all(T, "l%s%d" % (k, s), k)


def _away(T, topo, src, s, k):
    dests = _plan(topo, s, k)[src]
    m = _off_mask(topo, src, dests)
    return RemoteDMATransfer(dst_ids=[_dst(topo, src, CORES[d]) for d in dests], dma_engine_mask=m,
                             remote_sem=T.sem["r%s%d" % (k, s)], srcs=[_all(T, "d" + k, k)],
                             dsts=[_land(T, s, k, d) for d in dests], alu_op=0), len(_bits(m))


def _came(topo, r, s, k):
    for src, dests in _plan(topo, s, k).items():
        if r in dests:
            return len(_bits(_off_mask(topo, src, dests)))


def rank_program(g, core, T, topo):
    rank = T.rank_of(core)
    if rank is not None:
        _sends(g, core, T, topo, rank)
        _compute(g, core, T, topo, rank)
        return
    for s in range(N):
        if core in _helpers(topo, s):
            _helper(g, core, T, topo, s)


def _helper(g, core, T, topo, s):
    sent = 0
    for k in "paqbrc" if s < G else "rc":
        if _plan(topo, s, k)[core]:
            g.wait_ge(T.sem["h" + k], len(_bits(_chip_mask(topo, CORES[s], core))))
            t, e = _away(T, topo, core, s, k)
            g.remote_dma_fused([t], local_sem=T.sem.out)
            sent += e
    if sent:
        g.wait_ge(T.sem.out, sent)


def _sends(g, core, T, topo, r):
    sem = T.sem
    sent = [0]

    def inside(k):
        to = [h for h in _helpers(topo, r) if _plan(topo, r, k)[h]]
        if to:
            m = _chip_mask(topo, core, to[0])
            sent[0] += len(_bits(m))
            d = _all(T, "d" + k, k)
            g.remote_dma_fused([RemoteDMATransfer(dst_ids=[_dst(topo, core, h) for h in to], dma_engine_mask=m,
                                                  remote_sem=sem["h" + k], srcs=[d], dsts=[d for h in to],
                                                  alu_op=0)], local_sem=sem.out)

    def away(k):
        if _plan(topo, r, k)[core]:
            t, e = _away(T, topo, core, r, k)
            sent[0] += e
            g.remote_dma_fused([t], local_sem=sem.out)

    def mate(src, plane, codes, name, local):
        m = _mate_mask(topo, r)
        to = _dst(topo, core, CORES[MATE[r]])
        for s, d, n in ((T["s" + src][:], plane[:], name + "p"), (_u8(T["q" + src]), _u8(codes), name + "c")):
            if local == "out":
                sent[0] += len(_bits(m))
            g.remote_dma_fused([RemoteDMATransfer(dst_ids=[to], dma_engine_mask=m, remote_sem=sem[n], srcs=[s], dsts=[d],
                                                  alu_op=0)], local_sem=sem[local])

    first = LAYER[r] == "a"
    if r < G:
        g.wait_ge(sem.sp, 16)
        inside("p")
        g.wait_ge(sem.sa, 16)
        inside("a")
    if not first:
        g.wait_ge(sem.qx, 1)
        mate("x", T.so, T.qo, "o", "out")
    if r < G:
        away("p")
        away("a")
        g.wait_ge(sem.sq, 16)
        inside("q")
        away("q")
        g.wait_ge(sem.sb, 16)
        inside("b")
        away("b")
    g.wait_ge(sem.sr, 16)
    inside("r")
    g.wait_ge(sem.sc, 16)
    inside("c")
    g.wait_ge(sem.q0, 1)
    if first:
        mate("v", T.sv, T.qv, "v", "out")
        g.wait_ge(sem.q1, 1)
        mate("w", T.lh, T.lg, "w", "out")
    else:
        mate("h", T.sh, T.qh, "k", "gone")
    g.wait_ge(sem.out, sent[0])


def _compute(g, core, T, topo, r):
    sem, sync, scalar, vector, tensor = T.sem, g.sync, g.scalar, g.vector, g.tensor
    k = LAYER[r]
    first = k == "a"
    got = len(_bits(_mate_mask(topo, MATE[r])))

    order, places = ORDER[r], PLACES[k]
    order_c = []
    for p in [(r // 2 - i) % (N // 2) for i in range(N // 2)]:
        order_c += [2 * p, 2 * p + 1] if 2 * p + 1 != r else [2 * p + 1, 2 * p]

    def tile(i):
        s, p = order[i], places[i]
        if s in LANDED[r]:
            return
        for q, n, x, own in ((sync, "lw", k, T.ac if first else T.bc), (scalar, "nw", PLANE[k], T.az if first else T.bs)):
            if s == r:
                src = own[:]
            else:
                q.wait_ge(sem["r%s%d" % (x, s)], _came(topo, r, s, x))
                src = _land(T, s, x, r)
            for m in [m for m in range(i) if places[m] == p]:
                q.wait_ge(sem["m0%d" % m], 1)
                q.wait_ge(sem["m1%d" % m], 1)
            q.dma_start(_place8(T, p, r, q is sync), src).then_inc(sem["%s%d" % (n, i)], 16)

    def tile_c(i):
        s, w = order_c[i], slice(W * (i % 2), W * (i % 2) + W)
        for q, n, x, buf, own in ((sync, "lc", "c", T.wc[:, w].bitcast(dt.uint8), T.cc),
                                  (scalar, "nc", "r", T.pc[:, w], T.cs)):
            if s == r:
                src = own[:]
            else:
                q.wait_ge(sem["r%s%d" % (x, s)], _came(topo, r, s, x))
                src = _land(T, s, x, r)
            if i >= 2:
                q.wait_ge(sem["mc%d" % (i - 2)], 1)
            q.dma_start(buf, src).then_inc(sem["%s%d" % (n, i)], 16)

    def block(q, i):
        a, b = W * (i % 2), 512 * (i % 2)
        q.wait_ge(sem["mc%d" % i], 1)
        if i >= 2:
            q.wait_ge(sem["y%d" % (i - 2)], 16)
        if q is vector:
            c = q.tensor_copy(T.yb[:, a:a + W], T.zc[:, b:b + W])
        else:
            c = q.activation(T.yb[:, a:a + W], T.zc[:, b:b + W], ActivationFunctionType.Copy)
        c.then_inc(sem["ec%d" % i], 1)

    def store(q, i):
        a, s = W * (i % 2), W * order_c[i]
        q.wait_ge(sem["ec%d" % i], 1)
        q.dma_start(T.y[:, s:s + W], T.yb[:, a:a + W]).then_inc(sem["y%d" % i], 16)

    if r < G:
        sync.dma_start(_u8(T.da), T.ac[:]).then_inc(sem.sa, 16)
        scalar.dma_start(T.dp[:], T.az[:]).then_inc(sem.sp, 16)
    scalar.dma_start(T.tx[:], T.x[:]).then_inc(sem.lx, 16)
    if r < G and first:
        tile(0)
    if r < G:
        sync.dma_start(_u8(T.db), T.bc[:]).then_inc(sem.sb, 16)
        scalar.dma_start(T.dq[:], T.bs[:]).then_inc(sem.sq, 16)
    sync.dma_start(_u8(T.dc), T.cc[:]).then_inc(sem.sc, 16)
    scalar.dma_start(T.dr[:], T.cs[:]).then_inc(sem.sr, 16)
    if r < G and not first:
        tile(0)
    if first:
        for i in range(1, G):
            tile(i)
    tile_c(0)
    tile_c(1)
    if not first:
        for q, n, x, buf, src in ((sync, "lg", "wc", _u8(T.qv), _u8(T.lg)), (scalar, "ng", "wp", T.sv[:], T.lh[:])):
            q.wait_ge(sem[x], got)
            for i in range(G):
                q.wait_ge(sem["m0%d" % i], 1)
            q.dma_start(buf, src).then_inc(sem[n], 16)
    for i in range(0, N, 2):
        if i + 2 < N:
            tile_c(i + 2)
            tile_c(i + 3)
        store(sync, i)
        block(scalar, i + 1)
        store(scalar, i + 1)
    for i in range(N):
        sync.wait_ge(sem["y%d" % i], 16)

    vector.wait_ge(sem.lx, 16)
    vector.quantize_mx(T.qx[:], T.sx[:], T.tx[:]).then_inc(sem.qx, 1)
    out = "vw" if first else "hh"
    for j in range(2):
        z, banks = (T.z0, T.z1)[j], (2, 4)[j]
        if j:
            vector.wait_ge(sem.q0, 1)
        for i in range(G):
            s, b = order[i], 512 * (i % banks)
            vector.wait_ge(sem["m%d%d" % (j, i)], 1)
            vector.tensor_scalar(T.tt[:, s:4 * W:4], z[:, b:b + W], 0.0, SCALE, AluOpType.max,
                                 AluOpType.mult).then_inc(sem["e%d%d" % (j, i)], 1)
        for i in range(G):
            vector.wait_ge(sem["e%d%d" % (j, i)], 1)
        if j and not first:
            vector.wait_ge(sem.gone, 2 * len(_bits(_mate_mask(topo, r))))
        vector.quantize_mx(T["q" + out[j]][:], T["s" + out[j]][:], T.tt[:]).then_inc(sem["q%d" % j], 1)
    for i in range(0, N, 2):
        block(vector, i)

    moving = "xo" if first else "vv"
    steps = ((0, 0), (0, 1), (1, 0), (1, 1), (2, 0), (3, 0), (2, 1), (3, 1)) if first else (
        (0, 0), (1, 0), (2, 0), (3, 0), (0, 1), (1, 1), (2, 1), (3, 1))
    seen = []
    for i, j in steps:
        if j not in seen:
            seen.append(j)
            if first and j == 0:
                tensor.wait_ge(sem.qx, 1)
            elif first or j == 0:
                n = "o" if first else "v"
                tensor.wait_ge(sem[n + "p"], got)
                tensor.wait_ge(sem[n + "c"], got)
            else:
                tensor.wait_ge(sem.ng, 16)
                tensor.wait_ge(sem.lg, 16)
        s, p = order[i], places[i]
        if j == 0:
            if s in LANDED[r]:
                for x in (PLANE[k], k):
                    tensor.wait_ge(sem["r%s%d" % (x, s)], _came(topo, r, s, x))
            else:
                tensor.wait_ge(sem["nw%d" % i], 16)
                tensor.wait_ge(sem["lw%d" % i], 16)
        z, banks = (T.z0, T.z1)[j], (2, 4)[j]
        if i >= banks:
            tensor.wait_ge(sem["e%d%d" % (j, i - banks)], 1)
        b = 512 * (i % banks)
        tensor.matmul_mx(z[:, b:b + W], _place(T, p, r, True), _place(T, p, r, False), T["q" + moving[j]][:],
                         T["s" + moving[j]][:], True, True).then_inc(sem["m%d%d" % (j, i)], 1)
    if first:
        tensor.wait_ge(sem.kp, got)
        tensor.wait_ge(sem.kc, got)
    else:
        tensor.wait_ge(sem.q1, 1)
    for i in range(N):
        w, b = slice(W * (i % 2), W * (i % 2) + W), 512 * (i % 2)
        tensor.wait_ge(sem["nc%d" % i], 16)
        tensor.wait_ge(sem["lc%d" % i], 16)
        if i >= 2:
            tensor.wait_ge(sem["ec%d" % (i - 2)], 1)
        tensor.matmul_mx(T.zc[:, b:b + W], T.wc[:, w], T.pc[:, w], T.qh[:], T.sh[:], True, True).then_inc(sem["mc%d" % i], 1)
